import numpy as np
import ml_dtypes


def mxq(x, axis, fmt="e4m3"):
    dtype, down = {"e4m3": (ml_dtypes.float8_e4m3fn, 7), "e5m2": (ml_dtypes.float8_e5m2, 14)}[fmt]
    v = np.moveaxis(np.asarray(x, np.float32).astype(ml_dtypes.bfloat16).astype(np.float64), axis, -1)
    blocks = v.reshape(v.shape[:-1] + (-1, 32))
    amax = np.abs(blocks).max(-1, keepdims=True)
    byte = np.maximum(np.where(amax > 0, np.frexp(amax)[1] - 1 + 127, 0) - down, 1)
    scale = np.exp2(byte - 127.0)
    codes = (blocks / scale).astype(np.float32).astype(dtype).astype(np.float64)
    return np.moveaxis((codes * scale).reshape(v.shape), -1, axis)


WIDE = False


def mx_kscale(k):
    if not WIDE:
        return np.ones(k)
    levels = np.array([10, -10, 5, -5, 0])
    if k % 512:
        return np.exp2(np.random.permutation(np.resize(levels, k // 32))).repeat(32)
    a = np.empty((k // 512, 16))
    for p in range(k // 512):
        a[p, :8] = np.random.permutation(np.resize(levels, 8))
        for g in range(8):
            far = levels[np.abs(levels - a[p, g]) >= 10]
            a[p, g + 8] = far[np.random.randint(len(far))]
    return np.exp2(a.ravel()).repeat(32)


def f64(x):
    return np.asarray(x).astype(np.float64)


def striped(idx):
    return np.tile(idx.reshape(-1, 16).T, (8, 1)).astype(np.uint16)


def unstriped(offs):
    return offs[:16].T.reshape(-1).astype(np.int64)


def pack_weight(w):
    k, n = w.shape
    w = f64(np.asarray(w, np.float32).astype(ml_dtypes.bfloat16)).reshape(k // 32, 32, n)
    amax = np.abs(w).max(1)
    byte = np.clip(np.where(amax > 0, np.frexp(amax)[1] - 1 + 127 - 7, 1), 1, 254)
    scaled = (w * np.exp2(127.0 - byte)[:, None, :]).reshape(k, n).astype(np.float32)
    words = np.ascontiguousarray(scaled.reshape(k // 512, 128, 4, n).transpose(0, 1, 3, 2)).astype(ml_dtypes.float8_e4m3fn).view(np.uint8)
    return words, np.ascontiguousarray(byte.astype(np.uint8).reshape(k // 512, 16, n))


def unpack_weight(words, scales):
    g, p, n, _ = words.shape
    vals = np.ascontiguousarray(words).view(ml_dtypes.float8_e4m3fn).astype(np.float64) * np.repeat(np.exp2(scales.astype(np.float64) - 127.0), 8, axis=1)[..., None]
    return vals.transpose(0, 1, 3, 2).reshape(g * 512, n)


K, T, S, N, U, D, V, R = 1024, 2048, 512, 128, 512, 4, 128, 256
P = 2 ** 7


def setup_inputs():
    n = np.random.standard_normal
    s = mx_kscale(K)[:, None]
    packed_xT = pack_weight(n((K, T)) * s)
    return {
        "x_words": packed_xT[0],
        "x_scales": packed_xT[1],
        "w1": (n((K, N)) / np.sqrt(K) / s).astype(np.float32),
        "att": (np.tile(np.random.uniform(0.2, 1.0, U), (P, 1))).astype(np.float32),
        "hand": (np.tile(np.random.uniform(0.1, 0.6, U), (P, 1))).astype(np.float32),
        "pred": (np.random.uniform(0.2, 1.5, (N, V))).astype(np.float32),
        "offs": striped(np.random.permutation(T)[:S]),
        "eats": striped(np.random.randint(0, S, U)),
        "linka": striped(np.random.permutation(U)[:R]),
        "linkb": striped(np.random.permutation(U)[:R]),
        "who": striped(np.random.permutation(S)[:R]),
    }


def reference(x_words, x_scales, w1, att, hand, pred, offs, eats, linka, linkb, who):
    xq = unpack_weight(x_words, x_scales)[:, unstriped(offs)]
    y = mxq(f64(w1), 0, "e4m3").T @ xq
    prey = np.exp(0.5 * y)
    own = prey[:, unstriped(who)]
    enc = prey[:, unstriped(eats)] * f64(att)[:1]
    gh = enc * f64(hand)[:1]
    busy = gh.reshape(len(gh), -1, D).sum(axis=2) + 1.0
    eat = enc / np.repeat(busy, D, axis=1)
    loss = eat * (np.repeat(f64(pred), D, axis=1))
    return own * (-1.0 * (0.4 * own) + 1.0) - loss[:, unstriped(linka)] - loss[:, unstriped(linkb)]

@@ -1,0 +1,153 @@
+import concourse.mybir as mybir
+
+F32 = mybir.dt.float32
+BF16 = mybir.dt.bfloat16
+I32 = mybir.dt.int32
+U32 = mybir.dt.uint32
+U16 = mybir.dt.uint16
+U8 = mybir.dt.uint8
+FP8X4 = mybir.dt.float8_e4m3fn_x4
+ALU = mybir.AluOpType
+ACT = mybir.ActivationFunctionType
+AX = mybir.AxisListType
+
+P = 128
+K, T, S, M, U, D, V, R = 1024, 2048, 512, 128, 512, 4, 128, 256
+PASSES = 2
+FLOPS = 2 * K * M * S
+
+
+def tile_picked_yholl_prey_p_kernel(
+    tc, x_words, x_scales, w1, att, hand, pred, offs, eats, linka, linkb, who, out
+):
+    nc = tc.nc
+    with tc.tile_pool(name="keep", bufs=1) as keep, tc.psum_pool(name="psum", bufs=1) as psum:
+        offs_t = keep.tile([P, S // 16], U16, name="offs_t")
+        eats_t = keep.tile([P, U // 16], U16, name="eats_t")
+        linka_t = keep.tile([P, R // 16], U16, name="linka_t")
+        linkb_t = keep.tile([P, R // 16], U16, name="linkb_t")
+        who_t = keep.tile([P, R // 16], U16, name="who_t")
+
+        w_raw = keep.tile([P, PASSES, 4, M], F32, name="w_raw")
+        nc.scalar.dma_start(w_raw[:], w1.rearrange("(o p j) m -> p o j m", o=PASSES, j=4))
+        nc.sync.dma_start(offs_t[:], offs)
+        words = [keep.tile([P, T], U32, name="words%d" % o) for o in range(PASSES)]
+        for o in range(PASSES):
+            nc.sync.dma_start(words[o][:].bitcast(I32), x_words[o].rearrange("p n t -> p (n t)").bitcast(I32))
+        planes = keep.tile([P, T], U8, name="planes", tag="planes", align_bytes=64)
+        nc.vector.memset(planes[:].bitcast(I32), 0)
+        for q in range(4):
+            nc.gpsimd.dma_start(
+                planes[32 * q : 32 * q + 8, :].bitcast(I32), x_scales[:, 4 * q : 4 * q + 4, :].bitcast(I32)
+            )
+        att_t = keep.tile([P, U], F32, name="att_t")
+        hand_t = keep.tile([P, U], F32, name="hand_t")
+        pred_t = keep.tile([P, V], F32, name="pred_t")
+        nc.sync.dma_start(eats_t[:], eats)
+        nc.sync.dma_start(att_t[:], att)
+        nc.sync.dma_start(hand_t[:], hand)
+        nc.sync.dma_start(who_t[:], who)
+        nc.sync.dma_start(pred_t[:], pred)
+        nc.sync.dma_start(linka_t[:], linka)
+        nc.sync.dma_start(linkb_t[:], linkb)
+
+        w_bf = keep.tile([P, PASSES, M, 4], BF16, name="w_bf", align_bytes=64)
+        nc.scalar.copy(w_bf[:], w_raw[:].rearrange("p o j m -> p o m j"))
+        w_codes = keep.tile([P, PASSES * M], U32, name="w_codes", align_bytes=64)
+        w_scales = keep.tile([P, PASSES * M], U8, name="w_scales", align_bytes=64)
+
+        x_sc = keep.tile([P, S], U8, name="x_sc", align_bytes=64)
+        nc.vector.tensor_copy(x_sc[:], planes[:].indirect(offs_t[:]))
+        x0 = keep.tile([P, S], U32, name="x0", align_bytes=64)
+        nc.vector.tensor_copy(x0[:], words[0][:].indirect(offs_t[:]))
+        nc.vector.quantize_mx(
+            out=w_codes[:].bitcast(FP8X4), scales=w_scales[:], in_=w_bf[:].rearrange("p o m j -> p (o m j)")
+        )
+        H = S // 2
+        ys = [psum.tile([P, H], F32, name="y%d" % h) for h in range(2)]
+        for h in range(2):
+            nc.tensor.matmul_mx(
+                out=ys[h][:],
+                lhsT=w_codes[:, 0:M].bitcast(FP8X4),
+                lhsT_scale=w_scales[:, 0:M],
+                rhs=x0[:, h * H : (h + 1) * H].bitcast(FP8X4),
+                rhs_scale=x_sc[:, h * H : (h + 1) * H],
+                start=True,
+                stop=False,
+            )
+        prey = keep.tile([P, S], F32, name="prey")
+        for h in range(2):
+            x1 = keep.tile([P, H], U32, name="x1_%d" % h, tag="planes" if h == 0 else "x1", align_bytes=64)
+            nc.vector.tensor_copy(x1[:], words[1][:].indirect(offs_t[:, 16 * h : 16 * h + 16]))
+            nc.tensor.matmul_mx(
+                out=ys[h][:],
+                lhsT=w_codes[:, M : 2 * M].bitcast(FP8X4),
+                lhsT_scale=w_scales[:, M : 2 * M],
+                rhs=x1[:].bitcast(FP8X4),
+                rhs_scale=x_sc[4:P, h * H : (h + 1) * H],
+                start=False,
+                stop=True,
+            )
+            nc.scalar.activation(prey[:, h * H : (h + 1) * H], ys[h][:], ACT.Exp, scale=0.5)
+
+        warm = keep.tile([P, 1], F32, name="warm")
+        nc.scalar.activation(warm[:], prey[:, S - 1 : S], ACT.Abs_reciprocal_sqrt)
+
+        VH = V // 2
+        enc = keep.tile([P, U], F32, name="enc")
+        gh = keep.tile([P, U], F32, name="gh")
+        tot = keep.tile([P, V], F32, name="tot")
+        sgn = keep.tile([P, V], F32, name="sgn")
+        root = keep.tile([P, V], F32, name="root")
+        inv = keep.tile([P, V], F32, name="inv")
+        spred = keep.tile([P, V], F32, name="spred")
+        fac = keep.tile([P, V], F32, name="fac")
+        nloss = keep.tile([P, U], F32, name="nloss")
+        own = keep.tile([P, R], F32, name="own")
+        room = keep.tile([P, R], F32, name="room")
+        grow = keep.tile([P, R], F32, name="grow")
+        part = keep.tile([P, R], F32, name="part")
+        cols = [slice(h * H, (h + 1) * H) for h in range(2)]
+        vs = [slice(h * VH, (h + 1) * VH) for h in range(2)]
+        for h in range(2):
+            nc.vector.tensor_tensor(
+                enc[:, cols[h]], prey[:].indirect(eats_t[:, 16 * h : 16 * h + 16]), att_t[:, cols[h]], ALU.mult
+            )
+        for h in range(2):
+            nc.vector.tensor_tensor(gh[:, cols[h]], enc[:, cols[h]], hand_t[:, cols[h]], ALU.mult)
+        for h in range(2):
+            nc.vector.tensor_reduce(
+                tot[:, vs[h]], gh[:, cols[h]].rearrange("p (v d) -> p v d", d=D), AX.X, ALU.add
+            )
+            nc.scalar.activation(sgn[:, vs[h]], tot[:, vs[h]], ACT.Sign, bias=1.0)
+            nc.scalar.activation(root[:, vs[h]], tot[:, vs[h]], ACT.Abs_reciprocal_sqrt, bias=1.0)
+            nc.scalar.activation(inv[:, vs[h]], root[:, vs[h]], ACT.Square)
+        nc.vector.tensor_copy(own[:], prey[:].indirect(who_t[:]))
+        nc.scalar.activation(room[:], own[:], ACT.Identity, bias=1.0, scale=-0.4)
+        for h in range(2):
+            nc.vector.scalar_tensor_tensor(
+                spred[:, vs[h]], sgn[:, vs[h]], -1.0, pred_t[:, vs[h]], ALU.mult, ALU.mult
+            )
+        for h in range(2):
+            nc.vector.tensor_tensor(fac[:, vs[h]], inv[:, vs[h]], spred[:, vs[h]], ALU.mult)
+        for h in range(2):
+            nc.vector.tensor_tensor(
+                nloss[:, cols[h]].rearrange("p (v d) -> p v d", d=D),
+                enc[:, cols[h]].rearrange("p (v d) -> p v d", d=D),
+                fac[:, vs[h]].unsqueeze(2).to_broadcast([P, VH, D]),
+                ALU.mult,
+            )
+        nc.vector.tensor_tensor(grow[:], own[:], room[:], ALU.mult)
+        RH = R // 2
+        for h in range(2):
+            e = slice(h * RH, (h + 1) * RH)
+            nc.vector.tensor_tensor(
+                part[:, e], nloss[:].indirect(linka_t[:, 8 * h : 8 * h + 8]), grow[:, e], ALU.add
+            )
+        for h in range(2):
+            e = slice(h * RH, (h + 1) * RH)
+            res = keep.tile([P, RH], F32, name="res%d" % h)
+            nc.vector.tensor_tensor(
+                res[:], nloss[:].indirect(linkb_t[:, 8 * h : 8 * h + 8]), part[:, e], ALU.add
+            )
+            (nc.scalar if h == 0 else nc.sync).dma_start(out[:, e], res[:])

@@ -1,4 +1,5 @@
 import concourse.mybir as mybir
+from concourse.masks import make_identity
 
 F32 = mybir.dt.float32
 BF16 = mybir.dt.bfloat16
@@ -29,40 +30,50 @@ def tile_picked_yholl_prey_p_kernel(
         who_t = keep.tile([P, R // 16], U16, name="who_t")
 
         w_raw = keep.tile([P, PASSES, 4, M], F32, name="w_raw")
-        nc.scalar.dma_start(w_raw[:], w1.rearrange("(o p j) m -> p o j m", o=PASSES, j=4))
-        nc.sync.dma_start(offs_t[:], offs)
-        words = [keep.tile([P, T], U32, name="words%d" % o) for o in range(PASSES)]
-        for o in range(PASSES):
-            nc.sync.dma_start(words[o][:].bitcast(I32), x_words[o].rearrange("p n t -> p (n t)").bitcast(I32))
+        nc.sync.dma_start(w_raw[:], w1.rearrange("(o p j) m -> p o j m", o=PASSES, j=4))
         planes = keep.tile([P, T], U8, name="planes", tag="planes", align_bytes=64)
         nc.vector.memset(planes[:].bitcast(I32), 0)
         for q in range(4):
-            nc.gpsimd.dma_start(
+            (nc.sync if q < 2 else nc.gpsimd).dma_start(
                 planes[32 * q : 32 * q + 8, :].bitcast(I32), x_scales[:, 4 * q : 4 * q + 4, :].bitcast(I32)
             )
-        att_t = keep.tile([P, U], F32, name="att_t")
-        hand_t = keep.tile([P, U], F32, name="hand_t")
+        nc.sync.dma_start(offs_t[:], offs)
+        att_c = keep.tile([P, D], F32, name="att_c")
+        hand_c = keep.tile([P, D], F32, name="hand_c")
         pred_t = keep.tile([P, V], F32, name="pred_t")
-        nc.sync.dma_start(eats_t[:], eats)
-        nc.sync.dma_start(att_t[:], att)
-        nc.sync.dma_start(hand_t[:], hand)
-        nc.sync.dma_start(who_t[:], who)
+        nc.sync.dma_start(att_c[:], att[0].rearrange("(v d) -> v d", d=D))
+        nc.sync.dma_start(hand_c[:], hand[0].rearrange("(v d) -> v d", d=D))
+        words = [keep.tile([P, T], U32, name="words%d" % o, tag="words%d" % o) for o in range(PASSES)]
+        nc.sync.dma_start(words[0][:].bitcast(I32), x_words[0].rearrange("p n t -> p (n t)").bitcast(I32))
+        nc.sync.dma_start(words[1][:].bitcast(I32), x_words[1].rearrange("p n t -> p (n t)").bitcast(I32))
         nc.sync.dma_start(pred_t[:], pred)
+        nc.sync.dma_start(eats_t[:], eats)
+        nc.sync.dma_start(who_t[:], who)
         nc.sync.dma_start(linka_t[:], linka)
         nc.sync.dma_start(linkb_t[:], linkb)
+
+        ident = keep.tile([P, P], F32, name="ident")
+        make_identity(nc, ident[:])
+        ah_c = keep.tile([P, D], F32, name="ah_c")
+        nc.vector.tensor_tensor(ah_c[:], att_c[:], hand_c[:], ALU.mult)
+        att_ps = psum.tile([P, D, V], F32, name="att_ps")
+        ah_ps = psum.tile([P, D, V], F32, name="ah_ps")
+        for d in range(D):
+            nc.tensor.transpose(att_ps[:, d, :], att_c[:, d : d + 1].to_broadcast([P, P]), ident[:])
+        for d in range(D):
+            nc.tensor.transpose(ah_ps[:, d, :], ah_c[:, d : d + 1].to_broadcast([P, P]), ident[:])
 
         w_bf = keep.tile([P, PASSES, M, 4], BF16, name="w_bf", align_bytes=64)
         nc.scalar.copy(w_bf[:], w_raw[:].rearrange("p o j m -> p o m j"))
         w_codes = keep.tile([P, PASSES * M], U32, name="w_codes", align_bytes=64)
         w_scales = keep.tile([P, PASSES * M], U8, name="w_scales", align_bytes=64)
-
-        x_sc = keep.tile([P, S], U8, name="x_sc", align_bytes=64)
-        nc.vector.tensor_copy(x_sc[:], planes[:].indirect(offs_t[:]))
-        x0 = keep.tile([P, S], U32, name="x0", align_bytes=64)
-        nc.vector.tensor_copy(x0[:], words[0][:].indirect(offs_t[:]))
         nc.vector.quantize_mx(
             out=w_codes[:].bitcast(FP8X4), scales=w_scales[:], in_=w_bf[:].rearrange("p o m j -> p (o m j)")
         )
+        x0 = keep.tile([P, S], U32, name="x0", align_bytes=64)
+        nc.vector.tensor_copy(x0[:], words[0][:].indirect(offs_t[:]))
+        x_sc = keep.tile([P, S], U8, name="x_sc", align_bytes=64)
+        nc.vector.tensor_copy(x_sc[:], planes[:].indirect(offs_t[:]))
         H = S // 2
         ys = [psum.tile([P, H], F32, name="y%d" % h) for h in range(2)]
         for h in range(2):
@@ -90,17 +101,22 @@ def tile_picked_yholl_prey_p_kernel(
             )
             nc.scalar.activation(prey[:, h * H : (h + 1) * H], ys[h][:], ACT.Exp, scale=0.5)
 
+
+        ap = keep.tile([P, V, D], F32, name="ap", tag="words1")
+        nc.vector.tensor_tensor(
+            ap[:], att_ps[:].rearrange("p d v -> p v d"), pred_t[:].unsqueeze(2).to_broadcast([P, V, D]), ALU.mult
+        )
         warm = keep.tile([P, 1], F32, name="warm")
         nc.scalar.activation(warm[:], prey[:, S - 1 : S], ACT.Abs_reciprocal_sqrt)
 
         VH = V // 2
+        eaten = keep.tile([P, U], F32, name="eaten")
         enc = keep.tile([P, U], F32, name="enc")
-        gh = keep.tile([P, U], F32, name="gh")
+        gh = keep.tile([P, V, D], F32, name="gh")
         tot = keep.tile([P, V], F32, name="tot")
         sgn = keep.tile([P, V], F32, name="sgn")
         root = keep.tile([P, V], F32, name="root")
         inv = keep.tile([P, V], F32, name="inv")
-        spred = keep.tile([P, V], F32, name="spred")
         fac = keep.tile([P, V], F32, name="fac")
         nloss = keep.tile([P, U], F32, name="nloss")
         own = keep.tile([P, R], F32, name="own")
@@ -110,26 +126,30 @@ def tile_picked_yholl_prey_p_kernel(
         cols = [slice(h * H, (h + 1) * H) for h in range(2)]
         vs = [slice(h * VH, (h + 1) * VH) for h in range(2)]
         for h in range(2):
+            nc.vector.tensor_copy(eaten[:, cols[h]], prey[:].indirect(eats_t[:, 16 * h : 16 * h + 16]))
+        for h in range(2):
             nc.vector.tensor_tensor(
-                enc[:, cols[h]], prey[:].indirect(eats_t[:, 16 * h : 16 * h + 16]), att_t[:, cols[h]], ALU.mult
+                gh[:, vs[h], :],
+                eaten[:, cols[h]].rearrange("p (v d) -> p v d", d=D),
+                ah_ps[:, :, vs[h]].rearrange("p d v -> p v d"),
+                ALU.mult,
             )
         for h in range(2):
-            nc.vector.tensor_tensor(gh[:, cols[h]], enc[:, cols[h]], hand_t[:, cols[h]], ALU.mult)
-        for h in range(2):
-            nc.vector.tensor_reduce(
-                tot[:, vs[h]], gh[:, cols[h]].rearrange("p (v d) -> p v d", d=D), AX.X, ALU.add
+            nc.gpsimd.tensor_tensor(
+                enc[:, cols[h]], eaten[:, cols[h]], ap[:, vs[h], :].rearrange("p v d -> p (v d)"), ALU.mult
             )
-            nc.scalar.activation(sgn[:, vs[h]], tot[:, vs[h]], ACT.Sign, bias=1.0)
+        for h in range(2):
+            nc.vector.tensor_reduce(tot[:, vs[h]], gh[:, vs[h], :], AX.X, ALU.add)
             nc.scalar.activation(root[:, vs[h]], tot[:, vs[h]], ACT.Abs_reciprocal_sqrt, bias=1.0)
+            nc.scalar.activation(sgn[:, vs[h]], tot[:, vs[h]], ACT.Sign, bias=1.0)
             nc.scalar.activation(inv[:, vs[h]], root[:, vs[h]], ACT.Square)
         nc.vector.tensor_copy(own[:], prey[:].indirect(who_t[:]))
         nc.scalar.activation(room[:], own[:], ACT.Identity, bias=1.0, scale=-0.4)
+
         for h in range(2):
             nc.vector.scalar_tensor_tensor(
-                spred[:, vs[h]], sgn[:, vs[h]], -1.0, pred_t[:, vs[h]], ALU.mult, ALU.mult
+                fac[:, vs[h]], inv[:, vs[h]], -1.0, sgn[:, vs[h]], ALU.mult, ALU.mult
             )
-        for h in range(2):
-            nc.vector.tensor_tensor(fac[:, vs[h]], inv[:, vs[h]], spred[:, vs[h]], ALU.mult)
         for h in range(2):
             nc.vector.tensor_tensor(
                 nloss[:, cols[h]].rearrange("p (v d) -> p v d", d=D),
@@ -137,6 +157,7 @@ def tile_picked_yholl_prey_p_kernel(
                 fac[:, vs[h]].unsqueeze(2).to_broadcast([P, VH, D]),
                 ALU.mult,
             )
+
         nc.vector.tensor_tensor(grow[:], own[:], room[:], ALU.mult)
         RH = R // 2
         for h in range(2):

@@ -30,14 +30,6 @@ def tile_picked_yholl_prey_p_kernel(
         who_t = keep.tile([P, R // 16], U16, name="who_t")
 
         w_raw = keep.tile([P, PASSES, 4, M], F32, name="w_raw")
-        nc.sync.dma_start(w_raw[:], w1.rearrange("(o p j) m -> p o j m", o=PASSES, j=4))
-        planes = keep.tile([P, T], U8, name="planes", tag="planes", align_bytes=64)
-        nc.vector.memset(planes[:].bitcast(I32), 0)
-        for q in range(4):
-            (nc.sync if q < 2 else nc.gpsimd).dma_start(
-                planes[32 * q : 32 * q + 8, :].bitcast(I32), x_scales[:, 4 * q : 4 * q + 4, :].bitcast(I32)
-            )
-        nc.sync.dma_start(offs_t[:], offs)
         att_c = keep.tile([P, D], F32, name="att_c")
         hand_c = keep.tile([P, D], F32, name="hand_c")
         pred_t = keep.tile([P, V], F32, name="pred_t")
@@ -45,6 +37,14 @@ def tile_picked_yholl_prey_p_kernel(
         nc.sync.dma_start(hand_c[:], hand[0].rearrange("(v d) -> v d", d=D))
         words = [keep.tile([P, T], U32, name="words%d" % o, tag="words%d" % o) for o in range(PASSES)]
         nc.sync.dma_start(words[0][:].bitcast(I32), x_words[0].rearrange("p n t -> p (n t)").bitcast(I32))
+        nc.sync.dma_start(offs_t[:], offs)
+        planes = keep.tile([P, T], U8, name="planes", tag="planes", align_bytes=64)
+        nc.vector.memset(planes[:].bitcast(I32), 0)
+        for q in range(4):
+            nc.sync.dma_start(
+                planes[32 * q : 32 * q + 8, :].bitcast(I32), x_scales[:, 4 * q : 4 * q + 4, :].bitcast(I32)
+            )
+        nc.sync.dma_start(w_raw[:], w1.rearrange("(o p j) m -> p o j m", o=PASSES, j=4))
         nc.sync.dma_start(words[1][:].bitcast(I32), x_words[1].rearrange("p n t -> p (n t)").bitcast(I32))
         nc.sync.dma_start(pred_t[:], pred)
         nc.sync.dma_start(eats_t[:], eats)
@@ -63,17 +63,17 @@ def tile_picked_yholl_prey_p_kernel(
         for d in range(D):
             nc.tensor.transpose(ah_ps[:, d, :], ah_c[:, d : d + 1].to_broadcast([P, P]), ident[:])
 
-        w_bf = keep.tile([P, PASSES, M, 4], BF16, name="w_bf", align_bytes=64)
+        w_bf = keep.tile([P, PASSES, M, 4], BF16, name="w_bf", tag="w_bf", align_bytes=64)
         nc.scalar.copy(w_bf[:], w_raw[:].rearrange("p o j m -> p o m j"))
-        w_codes = keep.tile([P, PASSES * M], U32, name="w_codes", align_bytes=64)
-        w_scales = keep.tile([P, PASSES * M], U8, name="w_scales", align_bytes=64)
-        nc.vector.quantize_mx(
-            out=w_codes[:].bitcast(FP8X4), scales=w_scales[:], in_=w_bf[:].rearrange("p o m j -> p (o m j)")
-        )
         x0 = keep.tile([P, S], U32, name="x0", align_bytes=64)
         nc.vector.tensor_copy(x0[:], words[0][:].indirect(offs_t[:]))
         x_sc = keep.tile([P, S], U8, name="x_sc", align_bytes=64)
         nc.vector.tensor_copy(x_sc[:], planes[:].indirect(offs_t[:]))
+        w_codes = keep.tile([P, PASSES * M], U32, name="w_codes", tag="planes", align_bytes=64)
+        w_scales = keep.tile([P, PASSES * M], U8, name="w_scales", align_bytes=64)
+        nc.vector.quantize_mx(
+            out=w_codes[:].bitcast(FP8X4), scales=w_scales[:], in_=w_bf[:].rearrange("p o m j -> p (o m j)")
+        )
         H = S // 2
         ys = [psum.tile([P, H], F32, name="y%d" % h) for h in range(2)]
         for h in range(2):
@@ -86,20 +86,28 @@ def tile_picked_yholl_prey_p_kernel(
                 start=True,
                 stop=False,
             )
+        x1 = keep.tile([P, S], U32, name="x1", tag="w_bf", align_bytes=64)
         prey = keep.tile([P, S], F32, name="prey")
+        room = keep.tile([P, S], F32, name="room")
+        growth = keep.tile([P, S], F32, name="growth")
         for h in range(2):
-            x1 = keep.tile([P, H], U32, name="x1_%d" % h, tag="planes" if h == 0 else "x1", align_bytes=64)
-            nc.vector.tensor_copy(x1[:], words[1][:].indirect(offs_t[:, 16 * h : 16 * h + 16]))
+            nc.vector.tensor_copy(x1[:, h * H : (h + 1) * H], words[1][:].indirect(offs_t[:, 16 * h : 16 * h + 16]))
             nc.tensor.matmul_mx(
                 out=ys[h][:],
                 lhsT=w_codes[:, M : 2 * M].bitcast(FP8X4),
                 lhsT_scale=w_scales[:, M : 2 * M],
-                rhs=x1[:].bitcast(FP8X4),
+                rhs=x1[:, h * H : (h + 1) * H].bitcast(FP8X4),
                 rhs_scale=x_sc[4:P, h * H : (h + 1) * H],
                 start=False,
                 stop=True,
             )
             nc.scalar.activation(prey[:, h * H : (h + 1) * H], ys[h][:], ACT.Exp, scale=0.5)
+            nc.scalar.activation(
+                room[:, h * H : (h + 1) * H], prey[:, h * H : (h + 1) * H], ACT.Identity, bias=1.0, scale=-0.4
+            )
+            nc.gpsimd.tensor_tensor(
+                growth[:, h * H : (h + 1) * H], prey[:, h * H : (h + 1) * H], room[:, h * H : (h + 1) * H], ALU.mult
+            )
 
 
         ap = keep.tile([P, V, D], F32, name="ap", tag="words1")
@@ -107,7 +115,7 @@ def tile_picked_yholl_prey_p_kernel(
             ap[:], att_ps[:].rearrange("p d v -> p v d"), pred_t[:].unsqueeze(2).to_broadcast([P, V, D]), ALU.mult
         )
         warm = keep.tile([P, 1], F32, name="warm")
-        nc.scalar.activation(warm[:], prey[:, S - 1 : S], ACT.Abs_reciprocal_sqrt)
+        nc.scalar.activation(warm[:], room[:, S - 1 : S], ACT.Abs_reciprocal_sqrt)
 
         VH = V // 2
         eaten = keep.tile([P, U], F32, name="eaten")
@@ -119,8 +127,6 @@ def tile_picked_yholl_prey_p_kernel(
         inv = keep.tile([P, V], F32, name="inv")
         fac = keep.tile([P, V], F32, name="fac")
         nloss = keep.tile([P, U], F32, name="nloss")
-        own = keep.tile([P, R], F32, name="own")
-        room = keep.tile([P, R], F32, name="room")
         grow = keep.tile([P, R], F32, name="grow")
         part = keep.tile([P, R], F32, name="part")
         cols = [slice(h * H, (h + 1) * H) for h in range(2)]
@@ -143,8 +149,7 @@ def tile_picked_yholl_prey_p_kernel(
             nc.scalar.activation(root[:, vs[h]], tot[:, vs[h]], ACT.Abs_reciprocal_sqrt, bias=1.0)
             nc.scalar.activation(sgn[:, vs[h]], tot[:, vs[h]], ACT.Sign, bias=1.0)
             nc.scalar.activation(inv[:, vs[h]], root[:, vs[h]], ACT.Square)
-        nc.vector.tensor_copy(own[:], prey[:].indirect(who_t[:]))
-        nc.scalar.activation(room[:], own[:], ACT.Identity, bias=1.0, scale=-0.4)
+        nc.vector.tensor_copy(grow[:], growth[:].indirect(who_t[:]))
 
         for h in range(2):
             nc.vector.scalar_tensor_tensor(
@@ -158,7 +163,6 @@ def tile_picked_yholl_prey_p_kernel(
                 ALU.mult,
             )
 
-        nc.vector.tensor_tensor(grow[:], own[:], room[:], ALU.mult)
         RH = R // 2
         for h in range(2):
             e = slice(h * RH, (h + 1) * RH)

@@ -13,9 +13,32 @@ ACT = mybir.ActivationFunctionType
 AX = mybir.AxisListType
 
 P = 128
-K, T, S, M, U, D, V, R = 1024, 2048, 512, 128, 512, 4, 128, 256
-PASSES = 2
-FLOPS = 2 * K * M * S
+K = 1024
+TABLE = 2048
+PREY = 512
+PATCHES = 128
+LINKS = 512
+PER = 4
+PREDATORS = LINKS // PER
+OUTS = 256
+PACK = 4
+PASSES = K // (P * PACK)
+QUADRANT = 32
+ROWS = 4
+STRIPE = 16
+HALVES = 2
+
+FLOPS = 2 * K * PATCHES * PREY
+BYTES = (
+    K * TABLE
+    + K // 32 * TABLE
+    + 4 * (K * PATCHES + 2 * LINKS + PATCHES * PREDATORS + PATCHES * OUTS)
+    + 2 * P * (PREY + LINKS + 3 * OUTS) // STRIPE
+)
+
+
+def half(h, width):
+    return slice(h * width // HALVES, (h + 1) * width // HALVES)
 
 
 def tile_picked_yholl_prey_p_kernel(
@@ -23,28 +46,29 @@ def tile_picked_yholl_prey_p_kernel(
 ):
     nc = tc.nc
     with tc.tile_pool(name="keep", bufs=1) as keep, tc.psum_pool(name="psum", bufs=1) as psum:
-        offs_t = keep.tile([P, S // 16], U16, name="offs_t")
-        eats_t = keep.tile([P, U // 16], U16, name="eats_t")
-        linka_t = keep.tile([P, R // 16], U16, name="linka_t")
-        linkb_t = keep.tile([P, R // 16], U16, name="linkb_t")
-        who_t = keep.tile([P, R // 16], U16, name="who_t")
+        offs_t = keep.tile([P, PREY // STRIPE], U16, name="offs_t")
+        eats_t = keep.tile([P, LINKS // STRIPE], U16, name="eats_t")
+        linka_t = keep.tile([P, OUTS // STRIPE], U16, name="linka_t")
+        linkb_t = keep.tile([P, OUTS // STRIPE], U16, name="linkb_t")
+        who_t = keep.tile([P, OUTS // STRIPE], U16, name="who_t")
 
-        w_raw = keep.tile([P, PASSES, 4, M], F32, name="w_raw")
-        att_c = keep.tile([P, D], F32, name="att_c")
-        hand_c = keep.tile([P, D], F32, name="hand_c")
-        pred_t = keep.tile([P, V], F32, name="pred_t")
-        nc.sync.dma_start(att_c[:], att[0].rearrange("(v d) -> v d", d=D))
-        nc.sync.dma_start(hand_c[:], hand[0].rearrange("(v d) -> v d", d=D))
-        words = [keep.tile([P, T], U32, name="words%d" % o, tag="words%d" % o) for o in range(PASSES)]
+        w_raw = keep.tile([P, PASSES, PACK, PATCHES], F32, name="w_raw")
+        att_c = keep.tile([P, PER], F32, name="att_c")
+        hand_c = keep.tile([P, PER], F32, name="hand_c")
+        pred_t = keep.tile([P, PREDATORS], F32, name="pred_t")
+        nc.sync.dma_start(att_c[:], att[0].rearrange("(v d) -> v d", d=PER))
+        nc.sync.dma_start(hand_c[:], hand[0].rearrange("(v d) -> v d", d=PER))
+        words = [keep.tile([P, TABLE], U32, name="words%d" % o, tag="words%d" % o) for o in range(PASSES)]
         nc.sync.dma_start(words[0][:].bitcast(I32), x_words[0].rearrange("p n t -> p (n t)").bitcast(I32))
         nc.sync.dma_start(offs_t[:], offs)
-        planes = keep.tile([P, T], U8, name="planes", tag="planes", align_bytes=64)
-        nc.vector.memset(planes[:].bitcast(I32), 0)
-        for q in range(4):
+        scale_rows = keep.tile([P, TABLE], U8, name="scale_rows", tag="scale_rows", align_bytes=64)
+        nc.vector.memset(scale_rows[:].bitcast(I32), 0)
+        for q in range(P // QUADRANT):
             nc.sync.dma_start(
-                planes[32 * q : 32 * q + 8, :].bitcast(I32), x_scales[:, 4 * q : 4 * q + 4, :].bitcast(I32)
+                scale_rows[QUADRANT * q : QUADRANT * q + PASSES * ROWS, :].bitcast(I32),
+                x_scales[:, ROWS * q : ROWS * (q + 1), :].bitcast(I32),
             )
-        nc.sync.dma_start(w_raw[:], w1.rearrange("(o p j) m -> p o j m", o=PASSES, j=4))
+        nc.sync.dma_start(w_raw[:], w1.rearrange("(o p j) m -> p o j m", o=PASSES, j=PACK))
         nc.sync.dma_start(words[1][:].bitcast(I32), x_words[1].rearrange("p n t -> p (n t)").bitcast(I32))
         nc.sync.dma_start(pred_t[:], pred)
         nc.sync.dma_start(eats_t[:], eats)
@@ -54,125 +78,130 @@ def tile_picked_yholl_prey_p_kernel(
 
         ident = keep.tile([P, P], F32, name="ident")
         make_identity(nc, ident[:])
-        ah_c = keep.tile([P, D], F32, name="ah_c")
+        ah_c = keep.tile([P, PER], F32, name="ah_c")
         nc.vector.tensor_tensor(ah_c[:], att_c[:], hand_c[:], ALU.mult)
-        att_ps = psum.tile([P, D, V], F32, name="att_ps")
-        ah_ps = psum.tile([P, D, V], F32, name="ah_ps")
-        for d in range(D):
+        att_ps = psum.tile([P, PER, PREDATORS], F32, name="att_ps")
+        ah_ps = psum.tile([P, PER, PREDATORS], F32, name="ah_ps")
+        for d in range(PER):
             nc.tensor.transpose(att_ps[:, d, :], att_c[:, d : d + 1].to_broadcast([P, P]), ident[:])
-        for d in range(D):
+        for d in range(PER):
             nc.tensor.transpose(ah_ps[:, d, :], ah_c[:, d : d + 1].to_broadcast([P, P]), ident[:])
 
-        w_bf = keep.tile([P, PASSES, M, 4], BF16, name="w_bf", tag="w_bf", align_bytes=64)
-        nc.scalar.copy(w_bf[:], w_raw[:].rearrange("p o j m -> p o m j"))
-        x0 = keep.tile([P, S], U32, name="x0", align_bytes=64)
+        w_bf = keep.tile([P, PASSES, PATCHES, PACK], BF16, name="w_bf", tag="w_bf", align_bytes=64)
+        x0 = keep.tile([P, PREY], U32, name="x0", align_bytes=64)
         nc.vector.tensor_copy(x0[:], words[0][:].indirect(offs_t[:]))
-        x_sc = keep.tile([P, S], U8, name="x_sc", align_bytes=64)
-        nc.vector.tensor_copy(x_sc[:], planes[:].indirect(offs_t[:]))
-        w_codes = keep.tile([P, PASSES * M], U32, name="w_codes", tag="planes", align_bytes=64)
-        w_scales = keep.tile([P, PASSES * M], U8, name="w_scales", align_bytes=64)
+        x_sc = keep.tile([P, PREY], U8, name="x_sc", align_bytes=64)
+        nc.vector.tensor_copy(x_sc[:], scale_rows[:].indirect(offs_t[:]))
+
+        nc.scalar.copy(w_bf[:, 0], w_raw[:, 0].rearrange("p j m -> p m j"))
+        nc.vector.tensor_copy(w_bf[:, 1], w_raw[:, 1].rearrange("p j m -> p m j"))
+        w_codes = keep.tile([P, PASSES * PATCHES], U32, name="w_codes", tag="scale_rows", align_bytes=64)
+        w_scales = keep.tile([P, PASSES * PATCHES], U8, name="w_scales", align_bytes=64)
         nc.vector.quantize_mx(
             out=w_codes[:].bitcast(FP8X4), scales=w_scales[:], in_=w_bf[:].rearrange("p o m j -> p (o m j)")
         )
-        H = S // 2
-        ys = [psum.tile([P, H], F32, name="y%d" % h) for h in range(2)]
-        for h in range(2):
+
+        picks = [half(h, PREY) for h in range(HALVES)]
+        ys = [psum.tile([P, PREY // HALVES], F32, name="y%d" % h) for h in range(HALVES)]
+        for h in range(HALVES):
             nc.tensor.matmul_mx(
                 out=ys[h][:],
-                lhsT=w_codes[:, 0:M].bitcast(FP8X4),
-                lhsT_scale=w_scales[:, 0:M],
-                rhs=x0[:, h * H : (h + 1) * H].bitcast(FP8X4),
-                rhs_scale=x_sc[:, h * H : (h + 1) * H],
+                lhsT=w_codes[:, 0:PATCHES].bitcast(FP8X4),
+                lhsT_scale=w_scales[:, 0:PATCHES],
+                rhs=x0[:, picks[h]].bitcast(FP8X4),
+                rhs_scale=x_sc[:, picks[h]],
                 start=True,
                 stop=False,
             )
-        x1 = keep.tile([P, S], U32, name="x1", tag="w_bf", align_bytes=64)
-        prey = keep.tile([P, S], F32, name="prey")
-        room = keep.tile([P, S], F32, name="room")
-        growth = keep.tile([P, S], F32, name="growth")
-        for h in range(2):
-            nc.vector.tensor_copy(x1[:, h * H : (h + 1) * H], words[1][:].indirect(offs_t[:, 16 * h : 16 * h + 16]))
+        x1 = keep.tile([P, PREY], U32, name="x1", tag="w_bf", align_bytes=64)
+        prey = keep.tile([P, PREY], F32, name="prey")
+        room = keep.tile([P, PREY], F32, name="room")
+        growth = keep.tile([P, PREY], F32, name="growth")
+        for h in range(HALVES):
+            nc.vector.tensor_copy(x1[:, picks[h]], words[1][:].indirect(offs_t[:, half(h, PREY // STRIPE)]))
             nc.tensor.matmul_mx(
                 out=ys[h][:],
-                lhsT=w_codes[:, M : 2 * M].bitcast(FP8X4),
-                lhsT_scale=w_scales[:, M : 2 * M],
-                rhs=x1[:, h * H : (h + 1) * H].bitcast(FP8X4),
-                rhs_scale=x_sc[4:P, h * H : (h + 1) * H],
+                lhsT=w_codes[:, PATCHES : 2 * PATCHES].bitcast(FP8X4),
+                lhsT_scale=w_scales[:, PATCHES : 2 * PATCHES],
+                rhs=x1[:, picks[h]].bitcast(FP8X4),
+                rhs_scale=x_sc[ROWS:P, picks[h]],
                 start=False,
                 stop=True,
             )
-            nc.scalar.activation(prey[:, h * H : (h + 1) * H], ys[h][:], ACT.Exp, scale=0.5)
-            nc.scalar.activation(
-                room[:, h * H : (h + 1) * H], prey[:, h * H : (h + 1) * H], ACT.Identity, bias=1.0, scale=-0.4
-            )
-            nc.gpsimd.tensor_tensor(
-                growth[:, h * H : (h + 1) * H], prey[:, h * H : (h + 1) * H], room[:, h * H : (h + 1) * H], ALU.mult
-            )
+            nc.scalar.activation(prey[:, picks[h]], ys[h][:], ACT.Exp, scale=0.5)
 
-
-        ap = keep.tile([P, V, D], F32, name="ap", tag="words1")
+        att_pred = keep.tile([P, PREDATORS, PER], F32, name="att_pred", tag="words1")
         nc.vector.tensor_tensor(
-            ap[:], att_ps[:].rearrange("p d v -> p v d"), pred_t[:].unsqueeze(2).to_broadcast([P, V, D]), ALU.mult
+            att_pred[:],
+            att_ps[:].rearrange("p d v -> p v d"),
+            pred_t[:].unsqueeze(2).to_broadcast([P, PREDATORS, PER]),
+            ALU.mult,
         )
-        warm = keep.tile([P, 1], F32, name="warm")
-        nc.scalar.activation(warm[:], room[:, S - 1 : S], ACT.Abs_reciprocal_sqrt)
 
-        VH = V // 2
-        eaten = keep.tile([P, U], F32, name="eaten")
-        enc = keep.tile([P, U], F32, name="enc")
-        gh = keep.tile([P, V, D], F32, name="gh")
-        tot = keep.tile([P, V], F32, name="tot")
-        sgn = keep.tile([P, V], F32, name="sgn")
-        root = keep.tile([P, V], F32, name="root")
-        inv = keep.tile([P, V], F32, name="inv")
-        fac = keep.tile([P, V], F32, name="fac")
-        nloss = keep.tile([P, U], F32, name="nloss")
-        grow = keep.tile([P, R], F32, name="grow")
-        part = keep.tile([P, R], F32, name="part")
-        cols = [slice(h * H, (h + 1) * H) for h in range(2)]
-        vs = [slice(h * VH, (h + 1) * VH) for h in range(2)]
-        for h in range(2):
-            nc.vector.tensor_copy(eaten[:, cols[h]], prey[:].indirect(eats_t[:, 16 * h : 16 * h + 16]))
-        for h in range(2):
+        nc.gpsimd.tensor_scalar(room[:, picks[0]], prey[:, picks[0]], -0.4, 1.0, ALU.mult, ALU.add)
+        nc.scalar.activation(room[:, picks[1]], prey[:, picks[1]], ACT.Identity, bias=1.0, scale=-0.4)
+        for h in range(HALVES):
+            nc.gpsimd.tensor_tensor(growth[:, picks[h]], prey[:, picks[h]], room[:, picks[h]], ALU.mult)
+
+        eaten = keep.tile([P, LINKS], F32, name="eaten")
+        taken = keep.tile([P, LINKS], F32, name="taken")
+        handled = keep.tile([P, PREDATORS, PER], F32, name="handled")
+        total = keep.tile([P, PREDATORS], F32, name="total")
+        sign = keep.tile([P, PREDATORS], F32, name="sign")
+        root = keep.tile([P, PREDATORS], F32, name="root")
+        inverse = keep.tile([P, PREDATORS], F32, name="inverse")
+        factor = keep.tile([P, PREDATORS], F32, name="factor")
+        neg_loss = keep.tile([P, LINKS], F32, name="neg_loss")
+        own_growth = keep.tile([P, OUTS], F32, name="own_growth")
+        part = keep.tile([P, OUTS], F32, name="part")
+        links = [half(h, LINKS) for h in range(HALVES)]
+        preds = [half(h, PREDATORS) for h in range(HALVES)]
+
+        for h in range(HALVES):
+            nc.vector.tensor_copy(eaten[:, links[h]], prey[:].indirect(eats_t[:, half(h, LINKS // STRIPE)]))
+        for h in range(HALVES):
             nc.vector.tensor_tensor(
-                gh[:, vs[h], :],
-                eaten[:, cols[h]].rearrange("p (v d) -> p v d", d=D),
-                ah_ps[:, :, vs[h]].rearrange("p d v -> p v d"),
+                handled[:, preds[h], :],
+                eaten[:, links[h]].rearrange("p (v d) -> p v d", d=PER),
+                ah_ps[:, :, preds[h]].rearrange("p d v -> p v d"),
                 ALU.mult,
             )
-        for h in range(2):
+        for h in range(HALVES):
             nc.gpsimd.tensor_tensor(
-                enc[:, cols[h]], eaten[:, cols[h]], ap[:, vs[h], :].rearrange("p v d -> p (v d)"), ALU.mult
-            )
-        for h in range(2):
-            nc.vector.tensor_reduce(tot[:, vs[h]], gh[:, vs[h], :], AX.X, ALU.add)
-            nc.scalar.activation(root[:, vs[h]], tot[:, vs[h]], ACT.Abs_reciprocal_sqrt, bias=1.0)
-            nc.scalar.activation(sgn[:, vs[h]], tot[:, vs[h]], ACT.Sign, bias=1.0)
-            nc.scalar.activation(inv[:, vs[h]], root[:, vs[h]], ACT.Square)
-        nc.vector.tensor_copy(grow[:], growth[:].indirect(who_t[:]))
-
-        for h in range(2):
-            nc.vector.scalar_tensor_tensor(
-                fac[:, vs[h]], inv[:, vs[h]], -1.0, sgn[:, vs[h]], ALU.mult, ALU.mult
-            )
-        for h in range(2):
-            nc.vector.tensor_tensor(
-                nloss[:, cols[h]].rearrange("p (v d) -> p v d", d=D),
-                enc[:, cols[h]].rearrange("p (v d) -> p v d", d=D),
-                fac[:, vs[h]].unsqueeze(2).to_broadcast([P, VH, D]),
+                taken[:, links[h]],
+                eaten[:, links[h]],
+                att_pred[:, preds[h], :].rearrange("p v d -> p (v d)"),
                 ALU.mult,
             )
 
-        RH = R // 2
-        for h in range(2):
-            e = slice(h * RH, (h + 1) * RH)
-            nc.vector.tensor_tensor(
-                part[:, e], nloss[:].indirect(linka_t[:, 8 * h : 8 * h + 8]), grow[:, e], ALU.add
+        for h in range(HALVES):
+            nc.vector.tensor_reduce(total[:, preds[h]], handled[:, preds[h], :], AX.X, ALU.add)
+            nc.scalar.activation(root[:, preds[h]], total[:, preds[h]], ACT.Abs_reciprocal_sqrt, bias=1.0)
+            nc.scalar.activation(sign[:, preds[h]], total[:, preds[h]], ACT.Sign, bias=1.0)
+            nc.scalar.activation(inverse[:, preds[h]], root[:, preds[h]], ACT.Square)
+        nc.vector.tensor_copy(own_growth[:], growth[:].indirect(who_t[:]))
+
+        for h in range(HALVES):
+            nc.vector.scalar_tensor_tensor(
+                factor[:, preds[h]], inverse[:, preds[h]], -1.0, sign[:, preds[h]], ALU.mult, ALU.mult
             )
-        for h in range(2):
-            e = slice(h * RH, (h + 1) * RH)
-            res = keep.tile([P, RH], F32, name="res%d" % h)
+        for h in range(HALVES):
             nc.vector.tensor_tensor(
-                res[:], nloss[:].indirect(linkb_t[:, 8 * h : 8 * h + 8]), part[:, e], ALU.add
+                neg_loss[:, links[h]].rearrange("p (v d) -> p v d", d=PER),
+                taken[:, links[h]].rearrange("p (v d) -> p v d", d=PER),
+                factor[:, preds[h]].unsqueeze(2).to_broadcast([P, PREDATORS // HALVES, PER]),
+                ALU.mult,
             )
-            (nc.scalar if h == 0 else nc.sync).dma_start(out[:, e], res[:])
+
+        for h in range(HALVES):
+            cols = half(h, OUTS)
+            nc.vector.tensor_tensor(
+                part[:, cols], neg_loss[:].indirect(linka_t[:, half(h, OUTS // STRIPE)]), own_growth[:, cols], ALU.add
+            )
+        for h, queue in enumerate((nc.scalar, nc.sync)):
+            cols = half(h, OUTS)
+            result = keep.tile([P, OUTS // HALVES], F32, name="result%d" % h)
+            nc.vector.tensor_tensor(
+                result[:], neg_loss[:].indirect(linkb_t[:, half(h, OUTS // STRIPE)]), part[:, cols], ALU.add
+            )
+            queue.dma_start(out[:, cols], result[:])

import concourse.mybir as mybir
from concourse.masks import make_identity

F32 = mybir.dt.float32
BF16 = mybir.dt.bfloat16
I32 = mybir.dt.int32
U32 = mybir.dt.uint32
U16 = mybir.dt.uint16
U8 = mybir.dt.uint8
FP8X4 = mybir.dt.float8_e4m3fn_x4
ALU = mybir.AluOpType
ACT = mybir.ActivationFunctionType
AX = mybir.AxisListType

P = 128
K = 1024
TABLE = 2048
PREY = 512
PATCHES = 128
LINKS = 512
PER = 4
PREDATORS = LINKS // PER
OUTS = 256
PACK = 4
PASSES = K // (P * PACK)
QUADRANT = 32
ROWS = 4
STRIPE = 16
HALVES = 2

FLOPS = 2 * K * PATCHES * PREY
BYTES = (
    K * TABLE
    + K // 32 * TABLE
    + 4 * (K * PATCHES + 2 * LINKS + PATCHES * PREDATORS + PATCHES * OUTS)
    + 2 * P * (PREY + LINKS + 3 * OUTS) // STRIPE
)


def half(h, width):
    return slice(h * width // HALVES, (h + 1) * width // HALVES)


def tile_picked_yholl_prey_p_kernel(
    tc, x_words, x_scales, w1, att, hand, pred, offs, eats, linka, linkb, who, out
):
    nc = tc.nc
    with tc.tile_pool(name="keep", bufs=1) as keep, tc.psum_pool(name="psum", bufs=1) as psum:
        offs_t = keep.tile([P, PREY // STRIPE], U16, name="offs_t")
        eats_t = keep.tile([P, LINKS // STRIPE], U16, name="eats_t")
        linka_t = keep.tile([P, OUTS // STRIPE], U16, name="linka_t")
        linkb_t = keep.tile([P, OUTS // STRIPE], U16, name="linkb_t")
        who_t = keep.tile([P, OUTS // STRIPE], U16, name="who_t")

        w_raw = keep.tile([P, PASSES, PACK, PATCHES], F32, name="w_raw")
        att_c = keep.tile([P, PER], F32, name="att_c")
        hand_c = keep.tile([P, PER], F32, name="hand_c")
        pred_t = keep.tile([P, PREDATORS], F32, name="pred_t")
        nc.sync.dma_start(att_c[:], att[0].rearrange("(v d) -> v d", d=PER))
        nc.sync.dma_start(hand_c[:], hand[0].rearrange("(v d) -> v d", d=PER))
        words = [keep.tile([P, TABLE], U32, name="words%d" % o, tag="words%d" % o) for o in range(PASSES)]
        nc.sync.dma_start(words[0][:].bitcast(I32), x_words[0].rearrange("p n t -> p (n t)").bitcast(I32))
        nc.sync.dma_start(offs_t[:], offs)
        scale_rows = keep.tile([P, TABLE], U8, name="scale_rows", tag="scale_rows", align_bytes=64)
        nc.vector.memset(scale_rows[:].bitcast(I32), 0)
        for q in range(P // QUADRANT):
            nc.sync.dma_start(
                scale_rows[QUADRANT * q : QUADRANT * q + PASSES * ROWS, :].bitcast(I32),
                x_scales[:, ROWS * q : ROWS * (q + 1), :].bitcast(I32),
            )
        nc.sync.dma_start(w_raw[:], w1.rearrange("(o p j) m -> p o j m", o=PASSES, j=PACK))
        nc.sync.dma_start(words[1][:].bitcast(I32), x_words[1].rearrange("p n t -> p (n t)").bitcast(I32))
        nc.sync.dma_start(pred_t[:], pred)
        nc.sync.dma_start(eats_t[:], eats)
        nc.sync.dma_start(who_t[:], who)
        nc.sync.dma_start(linka_t[:], linka)
        nc.sync.dma_start(linkb_t[:], linkb)

        ident = keep.tile([P, P], F32, name="ident")
        make_identity(nc, ident[:])
        ah_c = keep.tile([P, PER], F32, name="ah_c")
        nc.vector.tensor_tensor(ah_c[:], att_c[:], hand_c[:], ALU.mult)
        att_ps = psum.tile([P, PER, PREDATORS], F32, name="att_ps")
        ah_ps = psum.tile([P, PER, PREDATORS], F32, name="ah_ps")
        for d in range(PER):
            nc.tensor.transpose(att_ps[:, d, :], att_c[:, d : d + 1].to_broadcast([P, P]), ident[:])
        for d in range(PER):
            nc.tensor.transpose(ah_ps[:, d, :], ah_c[:, d : d + 1].to_broadcast([P, P]), ident[:])

        w_bf = keep.tile([P, PASSES, PATCHES, PACK], BF16, name="w_bf", tag="w_bf", align_bytes=64)
        x0 = keep.tile([P, PREY], U32, name="x0", align_bytes=64)
        nc.vector.tensor_copy(x0[:], words[0][:].indirect(offs_t[:]))
        x_sc = keep.tile([P, PREY], U8, name="x_sc", align_bytes=64)
        nc.vector.tensor_copy(x_sc[:], scale_rows[:].indirect(offs_t[:]))

        nc.scalar.copy(w_bf[:, 0], w_raw[:, 0].rearrange("p j m -> p m j"))
        nc.vector.tensor_copy(w_bf[:, 1], w_raw[:, 1].rearrange("p j m -> p m j"))
        w_codes = keep.tile([P, PASSES * PATCHES], U32, name="w_codes", tag="scale_rows", align_bytes=64)
        w_scales = keep.tile([P, PASSES * PATCHES], U8, name="w_scales", align_bytes=64)
        nc.vector.quantize_mx(
            out=w_codes[:].bitcast(FP8X4), scales=w_scales[:], in_=w_bf[:].rearrange("p o m j -> p (o m j)")
        )

        picks = [half(h, PREY) for h in range(HALVES)]
        ys = [psum.tile([P, PREY // HALVES], F32, name="y%d" % h) for h in range(HALVES)]
        for h in range(HALVES):
            nc.tensor.matmul_mx(
                out=ys[h][:],
                lhsT=w_codes[:, 0:PATCHES].bitcast(FP8X4),
                lhsT_scale=w_scales[:, 0:PATCHES],
                rhs=x0[:, picks[h]].bitcast(FP8X4),
                rhs_scale=x_sc[:, picks[h]],
                start=True,
                stop=False,
            )
        x1 = keep.tile([P, PREY], U32, name="x1", tag="w_bf", align_bytes=64)
        prey = keep.tile([P, PREY], F32, name="prey")
        room = keep.tile([P, PREY], F32, name="room")
        growth = keep.tile([P, PREY], F32, name="growth")
        for h in range(HALVES):
            nc.vector.tensor_copy(x1[:, picks[h]], words[1][:].indirect(offs_t[:, half(h, PREY // STRIPE)]))
            nc.tensor.matmul_mx(
                out=ys[h][:],
                lhsT=w_codes[:, PATCHES : 2 * PATCHES].bitcast(FP8X4),
                lhsT_scale=w_scales[:, PATCHES : 2 * PATCHES],
                rhs=x1[:, picks[h]].bitcast(FP8X4),
                rhs_scale=x_sc[ROWS:P, picks[h]],
                start=False,
                stop=True,
            )
            nc.scalar.activation(prey[:, picks[h]], ys[h][:], ACT.Exp, scale=0.5)

        att_pred = keep.tile([P, PREDATORS, PER], F32, name="att_pred", tag="words1")
        nc.vector.tensor_tensor(
            att_pred[:],
            att_ps[:].rearrange("p d v -> p v d"),
            pred_t[:].unsqueeze(2).to_broadcast([P, PREDATORS, PER]),
            ALU.mult,
        )

        nc.gpsimd.tensor_scalar(room[:, picks[0]], prey[:, picks[0]], -0.4, 1.0, ALU.mult, ALU.add)
        nc.scalar.activation(room[:, picks[1]], prey[:, picks[1]], ACT.Identity, bias=1.0, scale=-0.4)
        for h in range(HALVES):
            nc.gpsimd.tensor_tensor(growth[:, picks[h]], prey[:, picks[h]], room[:, picks[h]], ALU.mult)

        eaten = keep.tile([P, LINKS], F32, name="eaten")
        taken = keep.tile([P, LINKS], F32, name="taken")
        handled = keep.tile([P, PREDATORS, PER], F32, name="handled")
        total = keep.tile([P, PREDATORS], F32, name="total")
        sign = keep.tile([P, PREDATORS], F32, name="sign")
        root = keep.tile([P, PREDATORS], F32, name="root")
        inverse = keep.tile([P, PREDATORS], F32, name="inverse")
        factor = keep.tile([P, PREDATORS], F32, name="factor")
        neg_loss = keep.tile([P, LINKS], F32, name="neg_loss")
        own_growth = keep.tile([P, OUTS], F32, name="own_growth")
        part = keep.tile([P, OUTS], F32, name="part")
        links = [half(h, LINKS) for h in range(HALVES)]
        preds = [half(h, PREDATORS) for h in range(HALVES)]

        for h in range(HALVES):
            nc.vector.tensor_copy(eaten[:, links[h]], prey[:].indirect(eats_t[:, half(h, LINKS // STRIPE)]))
        for h in range(HALVES):
            nc.vector.tensor_tensor(
                handled[:, preds[h], :],
                eaten[:, links[h]].rearrange("p (v d) -> p v d", d=PER),
                ah_ps[:, :, preds[h]].rearrange("p d v -> p v d"),
                ALU.mult,
            )
        for h in range(HALVES):
            nc.gpsimd.tensor_tensor(
                taken[:, links[h]],
                eaten[:, links[h]],
                att_pred[:, preds[h], :].rearrange("p v d -> p (v d)"),
                ALU.mult,
            )

        for h in range(HALVES):
            nc.vector.tensor_reduce(total[:, preds[h]], handled[:, preds[h], :], AX.X, ALU.add)
            nc.scalar.activation(root[:, preds[h]], total[:, preds[h]], ACT.Abs_reciprocal_sqrt, bias=1.0)
            nc.scalar.activation(sign[:, preds[h]], total[:, preds[h]], ACT.Sign, bias=1.0)
            nc.scalar.activation(inverse[:, preds[h]], root[:, preds[h]], ACT.Square)
        nc.vector.tensor_copy(own_growth[:], growth[:].indirect(who_t[:]))

        for h in range(HALVES):
            nc.vector.scalar_tensor_tensor(
                factor[:, preds[h]], inverse[:, preds[h]], -1.0, sign[:, preds[h]], ALU.mult, ALU.mult
            )
        for h in range(HALVES):
            nc.vector.tensor_tensor(
                neg_loss[:, links[h]].rearrange("p (v d) -> p v d", d=PER),
                taken[:, links[h]].rearrange("p (v d) -> p v d", d=PER),
                factor[:, preds[h]].unsqueeze(2).to_broadcast([P, PREDATORS // HALVES, PER]),
                ALU.mult,
            )

        for h in range(HALVES):
            cols = half(h, OUTS)
            nc.vector.tensor_tensor(
                part[:, cols], neg_loss[:].indirect(linka_t[:, half(h, OUTS // STRIPE)]), own_growth[:, cols], ALU.add
            )
        for h, queue in enumerate((nc.scalar, nc.sync)):
            cols = half(h, OUTS)
            result = keep.tile([P, OUTS // HALVES], F32, name="result%d" % h)
            nc.vector.tensor_tensor(
                result[:], neg_loss[:].indirect(linkb_t[:, half(h, OUTS // STRIPE)]), part[:, cols], ALU.add
            )
            queue.dma_start(out[:, cols], result[:])
